import numpy as np
import ml_dtypes


def mxq(x, axis, fmt="e4m3"):
    dtype, down = {"e4m3": (ml_dtypes.float8_e4m3fn, 7), "e5m2": (ml_dtypes.float8_e5m2, 14)}[fmt]
    v = np.moveaxis(np.asarray(x, np.float32).astype(ml_dtypes.bfloat16).astype(np.float64), axis, -1)
    blocks = v.reshape(v.shape[:-1] + (-1, 32))
    amax = np.abs(blocks).max(-1, keepdims=True)
    byte = np.maximum(np.where(amax > 0, np.frexp(amax)[1] - 1 + 127, 0) - down, 1)
    scale = np.exp2(byte - 127.0)
    codes = (blocks / scale).astype(np.float32).astype(dtype).astype(np.float64)
    return np.moveaxis((codes * scale).reshape(v.shape), -1, axis)


WIDE = False


def mx_kscale(k):
    if not WIDE:
        return np.ones(k)
    levels = np.array([10, -10, 5, -5, 0])
    if k % 512:
        return np.exp2(np.random.permutation(np.resize(levels, k // 32))).repeat(32)
    a = np.empty((k // 512, 16))
    for p in range(k // 512):
        a[p, :8] = np.random.permutation(np.resize(levels, 8))
        for g in range(8):
            far = levels[np.abs(levels - a[p, g]) >= 10]
            a[p, g + 8] = far[np.random.randint(len(far))]
    return np.exp2(a.ravel()).repeat(32)


def f64(x):
    return np.asarray(x).astype(np.float64)


def striped(idx):
    return np.tile(idx.reshape(-1, 16).T, (8, 1)).astype(np.uint16)


def unstriped(offs):
    return offs[:16].T.reshape(-1).astype(np.int64)


def pack_weight(w):
    k, n = w.shape
    w = f64(np.asarray(w, np.float32).astype(ml_dtypes.bfloat16)).reshape(k // 32, 32, n)
    amax = np.abs(w).max(1)
    byte = np.clip(np.where(amax > 0, np.frexp(amax)[1] - 1 + 127 - 7, 1), 1, 254)
    scaled = (w * np.exp2(127.0 - byte)[:, None, :]).reshape(k, n).astype(np.float32)
    words = np.ascontiguousarray(scaled.reshape(k // 512, 128, 4, n).transpose(0, 1, 3, 2)).astype(ml_dtypes.float8_e4m3fn).view(np.uint8)
    return words, np.ascontiguousarray(byte.astype(np.uint8).reshape(k // 512, 16, n))


def unpack_weight(words, scales):
    g, p, n, _ = words.shape
    vals = np.ascontiguousarray(words).view(ml_dtypes.float8_e4m3fn).astype(np.float64) * np.repeat(np.exp2(scales.astype(np.float64) - 127.0), 8, axis=1)[..., None]
    return vals.transpose(0, 1, 3, 2).reshape(g * 512, n)


E2M1 = np.array([0.0, 0.5, 1.0, 1.5, 2.0, 3.0, 4.0, 6.0, -0.0, -0.5, -1.0, -1.5, -2.0, -3.0, -4.0, -6.0])


def pack_fp4(w):
    k, n = w.shape
    w = f64(np.asarray(w, np.float32).astype(ml_dtypes.bfloat16)).reshape(k // 32, 32, n)
    amax = np.abs(w).max(1)
    mant, ex = np.frexp(amax / 6.0)
    byte = np.clip(np.where(amax > 0, np.where(mant > 0.5, ex, ex - 1) + 127, 1), 1, 254)
    scaled = (w * np.exp2(127.0 - byte)[:, None, :]).reshape(k, n).astype(np.float32)
    c = np.ascontiguousarray(scaled.reshape(k // 512, 128, 4, n).transpose(0, 1, 3, 2)).astype(ml_dtypes.float4_e2m1fn).view(np.uint8) & 0xF
    words = (c[..., 0::2] | (c[..., 1::2] << 4)).reshape(k // 512, 128, 2 * n)
    return np.ascontiguousarray(words), np.ascontiguousarray(byte.astype(np.uint8).reshape(k // 512, 16, n))


def unpack_fp4(words, scales):
    g, _, n = scales.shape
    words = np.ascontiguousarray(words).reshape(g, 128, n, 2)
    nib = np.empty((g, 128, n, 4), np.uint8)
    nib[..., 0::2] = words & 0xF
    nib[..., 1::2] = words >> 4
    vals = E2M1[nib] * np.repeat(np.exp2(scales.astype(np.float64) - 127.0), 8, axis=1)[..., None]
    return vals.transpose(0, 1, 3, 2).reshape(g * 512, n)


def relu(v):
    return np.maximum(v, 0.0)


def sigmoid(v):
    return 1.0 / (1.0 + np.exp(-np.maximum(v, -700.0)))


K, T, S, D, H, Z, W = 512, 2048, 512, 2, 512, 512, 2048
P = 2 ** 7


def setup_inputs():
    n = np.random.standard_normal
    s = mx_kscale(K)[:, None]
    u = mx_kscale(H)
    packed_xT = pack_weight(n((K, T)) * s)
    packed_w1 = pack_fp4(n((K, H)) / np.sqrt(K) / s)
    packed_eT = pack_weight(n((K, W)) * s)
    packed_w2 = pack_fp4(n((K, H)) / np.sqrt(K) / s)
    return {
        "x_words": packed_xT[0],
        "x_scales": packed_xT[1],
        "w1_words": packed_w1[0],
        "w1_scales": packed_w1[1],
        "e_words": packed_eT[0],
        "e_scales": packed_eT[1],
        "w2_words": packed_w2[0],
        "w2_scales": packed_w2[1],
        "unit": (np.random.uniform(0.6, 1.4, (H, 1)) * u[:, None]).astype(np.float32),
        "unit2": (np.random.uniform(0.6, 1.4, (H, 1)) / np.sqrt(H) / u[:, None]).astype(np.float32),
        "gap": (np.tile(np.random.uniform(0.1, 0.6, W), (P, 1))).astype(np.float32),
        "offs": striped(np.random.permutation(T)[:S]),
        "tpl": striped(np.random.permutation(W)[:Z]),
        "nx": striped(np.random.permutation(Z)),
        "dg": striped(np.random.permutation(Z)),
    }


def reference(x_words, x_scales, w1_words, w1_scales, e_words, e_scales, w2_words, w2_scales, unit, unit2, gap, offs, tpl, nx, dg):
    xq = unpack_weight(x_words, x_scales)[:, unstriped(offs)]
    y = unpack_fp4(w1_words, w1_scales).T @ xq
    seg = y.reshape(len(y), -1, D).max(axis=2)
    hid = f64(unit) * seg
    e_tpl = unpack_weight(e_words, e_scales)[:, unstriped(tpl)]
    ye = unpack_fp4(w2_words, w2_scales).T @ e_tpl
    gat = sigmoid(ye[:, unstriped(nx)])
    ctx = ye * gat
    hid2 = f64(unit2) * ctx
    sc = mxq(hid, 0, "e4m3").T @ mxq(hid2, 0, "e4m3")
    sd = sc[:, unstriped(dg)]
    ext = relu(sd - (f64(gap)[:1][:, unstriped(tpl)]))
    opn = ext - (f64(gap)[:1][:, unstriped(tpl)])
    return np.maximum(sc, opn)

@@ -1,0 +1,229 @@
+from contextlib import ExitStack
+
+import concourse.mybir as mybir
+from concourse.masks import make_identity
+
+F32 = mybir.dt.float32
+BF16 = mybir.dt.bfloat16
+I32 = mybir.dt.int32
+U32 = mybir.dt.uint32
+U16 = mybir.dt.uint16
+U8 = mybir.dt.uint8
+FP8X4 = mybir.dt.float8_e4m3fn_x4
+FP4X4 = mybir.dt.float4_e2m1fn_x4
+ALU = mybir.AluOpType
+ACT = mybir.ActivationFunctionType
+
+P = 128
+PACK = 4
+TABLE = 2048
+PICKED = 512
+HIDDEN = 512
+SEGMENTS = 256
+HALF = 256
+SPARE = 32
+
+FLOPS = 2 * 512 * 512 * 512 * 2 + 2 * 512 * 256 * 512
+
+
+def load_scale_rows(queue, plane, rows, q):
+    four = rows[4 * q : 4 * q + 4, :].bitcast(I32)
+    queue.dma_start(
+        out=plane[32 * q : 32 * q + 32, :].bitcast(I32),
+        in_=four.unsqueeze(0).broadcast_to([8, 4, four.shape[1]]),
+    )
+
+
+def deal(nc, dealt, raw):
+    nc.vector.tensor_copy(
+        out=dealt[:].bitcast(I32).rearrange("p (t g w) -> p t g w", t=PACK, g=16),
+        in_=raw[:].bitcast(I32).rearrange("p (g t w) -> p t g w", t=PACK, g=16),
+    )
+
+
+def tile_picked_yproloc_opn_p_kernel(
+    tc, x_words, x_scales, w1_words, w1_scales, e_words, e_scales, w2_words, w2_scales, unit, unit2, gap, offs, tpl, nx, dg, out
+):
+    nc = tc.nc
+    with ExitStack() as ctx:
+        keep = ctx.enter_context(tc.tile_pool(name="keep", bufs=1))
+        reuse = ctx.enter_context(tc.tile_pool(name="reuse", bufs=1))
+        psum = ctx.enter_context(tc.psum_pool(name="psum", bufs=1))
+
+        offs_sb = keep.tile([P, PICKED // 16], U16, name="offs_sb")
+        tpl_sb = keep.tile([P, PICKED // 16], U16, name="tpl_sb")
+        nx_sb = keep.tile([P, PICKED // 16], U16, name="nx_sb")
+        dg_sb = keep.tile([P, PICKED // 16], U16, name="dg_sb")
+        e_tab = reuse.tile([P, TABLE], I32, name="e_tab", offset=0)
+        x_tab = reuse.tile([P, TABLE], I32, name="x_tab", offset=8192)
+        e_tab_sc = keep.tile([P, TABLE], U8, name="e_tab_sc")
+        x_tab_sc = keep.tile([P, TABLE], U8, name="x_tab_sc")
+        gap_tab = keep.tile([P, TABLE], F32, name="gap_tab")
+        w1_raw = keep.tile([P, 2 * HIDDEN], U8, name="w1_raw")
+        w2_raw = keep.tile([P, 2 * HIDDEN], U8, name="w2_raw")
+        w1_raw_sc = reuse.tile([P, HIDDEN], U8, name="w1_raw_sc", offset=16384 + 512)
+        w2_raw_sc = keep.tile([P, HIDDEN], U8, name="w2_raw_sc")
+        unit_blocks = keep.tile([P, 2, 32], F32, name="unit_blocks")
+        identity = keep.tile([P, P], F32, name="identity")
+        lane = keep.tile([P, 8], F32, name="lane")
+        sc_sb = [keep.tile([P, PICKED + SPARE], F32, name="sc_sb%d" % h) for h in range(2)]
+
+        for h in range(2):
+            nc.vector.memset(sc_sb[h][:, PICKED:], 0.0)
+
+        nc.sync.dma_start(tpl_sb[:], tpl)
+        for q in range(4):
+            load_scale_rows(nc.scalar if q % 2 == 0 else nc.sync, e_tab_sc, e_scales[0], q)
+        nc.scalar.dma_start(out=w2_raw[:].bitcast(I32), in_=w2_words[0].bitcast(I32))
+        load_scale_rows(nc.sync, w2_raw_sc, w2_scales[0], 0)
+        nc.scalar.dma_start(out=e_tab[:], in_=e_words[0].rearrange("p n t -> p (n t)").bitcast(I32))
+        for q in range(1, 4):
+            load_scale_rows(nc.sync, w2_raw_sc, w2_scales[0], q)
+        nc.sync.dma_start(nx_sb[:], nx)
+        for which, factors in enumerate((unit, unit2)):
+            blocks = factors.rearrange("(g i) o -> g (i o)", i=32)
+            nc.sync.dma_start(out=unit_blocks[:, which, :], in_=blocks.unsqueeze(1).broadcast_to([16, 8, 32]))
+        nc.sync.dma_start(offs_sb[:], offs)
+        for q in range(4):
+            load_scale_rows(nc.sync, x_tab_sc, x_scales[0], q)
+        nc.sync.dma_start(out=w1_raw[:].bitcast(I32), in_=w1_words[0].bitcast(I32))
+        nc.sync.dma_start(out=x_tab[:], in_=x_words[0].rearrange("p n t -> p (n t)").bitcast(I32))
+        for q in range(4):
+            load_scale_rows(nc.sync, w1_raw_sc, w1_scales[0], q)
+        nc.sync.dma_start(out=gap_tab[:], in_=gap)
+        nc.sync.dma_start(dg_sb[:], dg)
+
+        w1_w = reuse.tile([P, 2 * HIDDEN], U8, name="w1_w", align_bytes=64, offset=8192)
+        w2_w = keep.tile([P, 2 * HIDDEN], U8, name="w2_w", align_bytes=64)
+        w1_s = reuse.tile([P, HIDDEN], U8, name="w1_s", align_bytes=64, offset=8192 + 1024)
+        w2_s = reuse.tile([P, HIDDEN], U8, name="w2_s", align_bytes=64, offset=16384)
+        e_w = keep.tile([P, PICKED], I32, name="e_w", align_bytes=64)
+        x_w = keep.tile([P, PICKED], I32, name="x_w", align_bytes=64)
+        e_s = keep.tile([P, PICKED], U8, name="e_s", align_bytes=64)
+        x_s = reuse.tile([P, PICKED], U8, name="x_s", align_bytes=64, offset=16384)
+
+        make_identity(nc, identity[:])
+        nc.vector.tensor_reduce(lane[:], identity[:].rearrange("p (g j) -> p j g", j=8), mybir.AxisListType.X, ALU.add)
+        deal(nc, w2_w, w2_raw)
+        nc.vector.tensor_copy(e_s[:], e_tab_sc[:].indirect(tpl_sb[:]))
+        deal(nc, w2_s, w2_raw_sc)
+        nc.vector.tensor_copy(e_w[:].bitcast(U32), e_tab[:].bitcast(U32).indirect(tpl_sb[:]))
+
+        def first_product(name, w_w, w_s, g_w, g_s):
+            banks = []
+            for t in range(PACK):
+                bank = psum.tile([P, PICKED], F32, name="%s%d" % (name, t))
+                nc.tensor.matmul_mx(
+                    out=bank[:],
+                    lhsT=w_w[:, 2 * P * t : 2 * P * (t + 1)].bitcast(FP4X4),
+                    lhsT_scale=w_s[:, P * t : P * (t + 1)],
+                    rhs=g_w[:].bitcast(FP8X4),
+                    rhs_scale=g_s[:],
+                    start=True,
+                    stop=True,
+                )
+                banks.append(bank)
+            return banks
+
+        ye_ps = first_product("ye_ps", w2_w, w2_s, e_w, e_s)
+
+        picked_units = reuse.tile([P, 2 * PACK, 8], F32, name="picked_units", offset=128)
+        units = keep.tile([P, 2 * PACK], F32, name="units")
+        nc.vector.tensor_tensor(
+            picked_units[:],
+            unit_blocks[:].rearrange("p w (t j) -> p (w t) j", j=8),
+            lane[:].unsqueeze(1).broadcast_to([P, 2 * PACK, 8]),
+            ALU.mult,
+        )
+        nc.vector.tensor_reduce(units[:], picked_units[:], mybir.AxisListType.X, ALU.add)
+        unit_sb = units[:, :PACK]
+        unit2_sb = units[:, PACK:]
+        unit_abs = reuse.tile([P, PACK], F32, name="unit_abs", offset=0)
+        unit_neg = reuse.tile([P, PACK], F32, name="unit_neg", offset=64)
+        unit2_signed = keep.tile([P, PACK], F32, name="unit2_signed")
+        nc.vector.scalar_tensor_tensor(unit_abs[:], unit_sb, -1.0, unit_sb, ALU.mult, ALU.max)
+        nc.vector.tensor_scalar(unit_neg[:], unit_sb, 0.0, -2.0, ALU.is_lt, ALU.mult)
+        nc.vector.scalar_tensor_tensor(unit2_signed[:], unit_neg[:], 1.0, unit2_sb, ALU.add, ALU.mult)
+
+
+        ye = [keep.tile([P, PICKED], F32, name="ye%d" % t) for t in range(PACK)]
+        gat = keep.tile([P, PACK, PICKED], F32, name="gat")
+        hid2_rows = reuse.tile([P, PACK, PICKED], BF16, name="hid2_rows", offset=16384 + 512)
+
+        def gate(t):
+            for h in range(2):
+                nc.scalar.activation(
+                    gat[:, t, HALF * h : HALF * (h + 1)],
+                    ye[t][:].indirect(nx_sb[:, 16 * h : 16 * (h + 1)]),
+                    ACT.Sigmoid,
+                )
+
+        nc.vector.tensor_copy(ye[0][:], ye_ps[0][:])
+        gate(0)
+        nc.vector.tensor_copy(ye[1][:], ye_ps[1][:])
+        gate(1)
+        nc.vector.tensor_copy(ye[2][:], ye_ps[2][:])
+        nc.scalar.copy(ye[3][:], ye_ps[3][:])
+        gate(2)
+        gate(3)
+        nc.vector.tensor_copy(x_s[:], x_tab_sc[:].indirect(offs_sb[:]))
+        nc.vector.tensor_copy(x_w[:].bitcast(U32), x_tab[:].bitcast(U32).indirect(offs_sb[:]))
+        deal(nc, w1_w, w1_raw)
+        deal(nc, w1_s, w1_raw_sc)
+        y_ps = first_product("y_ps", w1_w, w1_s, x_w, x_s)
+        for t in range(PACK):
+            nc.vector.scalar_tensor_tensor(
+                hid2_rows[:, t, :], ye_ps[t][:], unit2_signed[:, t : t + 1], gat[:, t, :], ALU.mult, ALU.mult
+            )
+        hid2_bf = keep.tile([P, PICKED, PACK], BF16, name="hid2_bf", align_bytes=64)
+        nc.vector.tensor_copy(hid2_bf[:], hid2_rows[:].rearrange("p t e -> p e t"))
+
+        hid2_w = keep.tile([P, PICKED], U32, name="hid2_w", align_bytes=64)
+        hid2_s = keep.tile([P, PICKED], U8, name="hid2_s", align_bytes=64)
+        nc.vector.quantize_mx(out=hid2_w[:].bitcast(FP8X4), scales=hid2_s[:], in_=hid2_bf[:].rearrange("p e t -> p (e t)"))
+
+        y_bf = [keep.tile([P, 2, PACK, P], BF16, name="y_bf%d" % h) for h in range(2)]
+        for h in range(2):
+            for t in range(PACK):
+                nc.scalar.activation(
+                    y_bf[h][:, :, t, :],
+                    y_ps[t][:, HALF * h : HALF * (h + 1)].rearrange("p (v d) -> p d v", d=2),
+                    ACT.Copy,
+                    scale=unit_abs[:, t : t + 1],
+                )
+        gap2 = reuse.tile([P, PICKED], F32, name="gap2", offset=0)
+        nc.scalar.activation(gap2[:], gap_tab[:].indirect(tpl_sb[:]), ACT.Copy, scale=-2.0)
+
+        sc_ps = []
+        for h in range(2):
+            hid_rows = keep.tile([P, PACK, P], BF16, name="hid_rows%d" % h)
+            hid_bf = keep.tile([P, P, PACK], BF16, name="hid_bf%d" % h, align_bytes=64)
+            hid_w = keep.tile([P, P], U32, name="hid_w%d" % h, align_bytes=64)
+            hid_s = keep.tile([P, P], U8, name="hid_s%d" % h, align_bytes=64)
+            nc.vector.tensor_tensor(hid_rows[:], y_bf[h][:, 0], y_bf[h][:, 1], ALU.max)
+            nc.vector.tensor_copy(hid_bf[:], hid_rows[:].rearrange("p t v -> p v t"))
+            nc.vector.quantize_mx(out=hid_w[:].bitcast(FP8X4), scales=hid_s[:], in_=hid_bf[:].rearrange("p v t -> p (v t)"))
+            bank = psum.tile([P, PICKED], F32, name="ye_ps%d" % h)
+            nc.tensor.matmul_mx(
+                out=bank[:],
+                lhsT=hid_w[:].bitcast(FP8X4),
+                lhsT_scale=hid_s[:],
+                rhs=hid2_w[:].bitcast(FP8X4),
+                rhs_scale=hid2_s[:],
+                start=True,
+                stop=True,
+            )
+            sc_ps.append(bank)
+        floor = [keep.tile([P, PICKED], F32, name="floor%d" % h) for h in range(2)]
+        opened = [keep.tile([P, PICKED], F32, name="opened%d" % h) for h in range(2)]
+        result = [keep.tile([P, PICKED], F32, name="result%d" % h) for h in range(2)]
+        nc.scalar.copy(sc_sb[0][:, :PICKED], sc_ps[0][:])
+        nc.vector.scalar_tensor_tensor(floor[1][:], gap2[:], 0.5, sc_ps[1][:], ALU.mult, ALU.max)
+        nc.scalar.copy(sc_sb[1][:, :PICKED], sc_ps[1][:])
+        nc.vector.tensor_tensor(opened[0][:], sc_sb[0][:].indirect(dg_sb[:]), gap2[:], ALU.add)
+        nc.vector.scalar_tensor_tensor(floor[0][:], gap2[:], 0.5, sc_ps[0][:], ALU.mult, ALU.max)
+        nc.vector.tensor_tensor(result[0][:], opened[0][:], floor[0][:], ALU.max)
+        nc.sync.dma_start(out=out[0:P, :], in_=result[0][:])
+        nc.vector.tensor_tensor(opened[1][:], sc_sb[1][:].indirect(dg_sb[:]), gap2[:], ALU.add)
+        nc.vector.tensor_tensor(result[1][:], opened[1][:], floor[1][:], ALU.max)
+        nc.sync.dma_start(out=out[P : 2 * P, :], in_=result[1][:])

@@ -1,7 +1,6 @@
 from contextlib import ExitStack
 
 import concourse.mybir as mybir
-from concourse.masks import make_identity
 
 F32 = mybir.dt.float32
 BF16 = mybir.dt.bfloat16
@@ -21,7 +20,6 @@ PICKED = 512
 HIDDEN = 512
 SEGMENTS = 256
 HALF = 256
-SPARE = 32
 
 FLOPS = 2 * 512 * 512 * 512 * 2 + 2 * 512 * 256 * 512
 
@@ -32,6 +30,13 @@ def load_scale_rows(queue, plane, rows, q):
         out=plane[32 * q : 32 * q + 32, :].bitcast(I32),
         in_=four.unsqueeze(0).broadcast_to([8, 4, four.shape[1]]),
     )
+
+
+def load_scale_rows_wrapped(queue, plane, rows):
+    words = rows.bitcast(I32)
+    width = words.shape[1]
+    queue.dma_start(out=plane[0:98, :].bitcast(I32), in_=words[0:14, :].unsqueeze(0).broadcast_to([7, 14, width]))
+    queue.dma_start(out=plane[98:P, :].bitcast(I32), in_=words[14:16, :].unsqueeze(0).broadcast_to([15, 2, width]))
 
 
 def deal(nc, dealt, raw):
@@ -61,49 +66,46 @@ def tile_picked_yproloc_opn_p_kernel(
         gap_tab = keep.tile([P, TABLE], F32, name="gap_tab")
         w1_raw = keep.tile([P, 2 * HIDDEN], U8, name="w1_raw")
         w2_raw = keep.tile([P, 2 * HIDDEN], U8, name="w2_raw")
-        w1_raw_sc = reuse.tile([P, HIDDEN], U8, name="w1_raw_sc", offset=16384 + 512)
+        w1_raw_sc = reuse.tile([P, HIDDEN], U8, name="w1_raw_sc", offset=24576)
         w2_raw_sc = keep.tile([P, HIDDEN], U8, name="w2_raw_sc")
         unit_blocks = keep.tile([P, 2, 32], F32, name="unit_blocks")
-        identity = keep.tile([P, P], F32, name="identity")
+        distance = keep.tile([P, 8], I32, name="distance")
+        distance8 = keep.tile([P, 8], I32, name="distance8")
         lane = keep.tile([P, 8], F32, name="lane")
-        sc_sb = [keep.tile([P, PICKED + SPARE], F32, name="sc_sb%d" % h) for h in range(2)]
+        sc_sb = [keep.tile([P, PICKED], F32, name="sc_sb%d" % h) for h in range(2)]
 
-        for h in range(2):
-            nc.vector.memset(sc_sb[h][:, PICKED:], 0.0)
+        nc.gpsimd.iota(distance[:], [[-1, 8]], base=8, channel_multiplier=1)
+        nc.vector.tensor_scalar(distance8[:], distance[:], 7, None, ALU.bitwise_and)
+        nc.vector.tensor_scalar(lane[:], distance8[:], 0.0, None, ALU.is_equal)
 
         nc.sync.dma_start(tpl_sb[:], tpl)
         for q in range(4):
-            load_scale_rows(nc.scalar if q % 2 == 0 else nc.sync, e_tab_sc, e_scales[0], q)
-        nc.scalar.dma_start(out=w2_raw[:].bitcast(I32), in_=w2_words[0].bitcast(I32))
-        load_scale_rows(nc.sync, w2_raw_sc, w2_scales[0], 0)
-        nc.scalar.dma_start(out=e_tab[:], in_=e_words[0].rearrange("p n t -> p (n t)").bitcast(I32))
-        for q in range(1, 4):
-            load_scale_rows(nc.sync, w2_raw_sc, w2_scales[0], q)
+            load_scale_rows(nc.sync, e_tab_sc, e_scales[0], q)
         nc.sync.dma_start(nx_sb[:], nx)
+        nc.sync.dma_start(out=w2_raw[:].bitcast(I32), in_=w2_words[0].bitcast(I32))
+        nc.sync.dma_start(out=e_tab[:], in_=e_words[0].rearrange("p n t -> p (n t)").bitcast(I32))
+        for q in range(4):
+            load_scale_rows(nc.sync, x_tab_sc, x_scales[0], q)
+        nc.sync.dma_start(offs_sb[:], offs)
+        nc.sync.dma_start(out=x_tab[:], in_=x_words[0].rearrange("p n t -> p (n t)").bitcast(I32))
+        nc.sync.dma_start(out=w1_raw[:].bitcast(I32), in_=w1_words[0].bitcast(I32))
         for which, factors in enumerate((unit, unit2)):
             blocks = factors.rearrange("(g i) o -> g (i o)", i=32)
             nc.sync.dma_start(out=unit_blocks[:, which, :], in_=blocks.unsqueeze(1).broadcast_to([16, 8, 32]))
-        nc.sync.dma_start(offs_sb[:], offs)
-        for q in range(4):
-            load_scale_rows(nc.sync, x_tab_sc, x_scales[0], q)
-        nc.sync.dma_start(out=w1_raw[:].bitcast(I32), in_=w1_words[0].bitcast(I32))
-        nc.sync.dma_start(out=x_tab[:], in_=x_words[0].rearrange("p n t -> p (n t)").bitcast(I32))
-        for q in range(4):
-            load_scale_rows(nc.sync, w1_raw_sc, w1_scales[0], q)
         nc.sync.dma_start(out=gap_tab[:], in_=gap)
         nc.sync.dma_start(dg_sb[:], dg)
+        load_scale_rows_wrapped(nc.gpsimd, w2_raw_sc, w2_scales[0])
+        load_scale_rows_wrapped(nc.gpsimd, w1_raw_sc, w1_scales[0])
 
-        w1_w = reuse.tile([P, 2 * HIDDEN], U8, name="w1_w", align_bytes=64, offset=8192)
-        w2_w = keep.tile([P, 2 * HIDDEN], U8, name="w2_w", align_bytes=64)
-        w1_s = reuse.tile([P, HIDDEN], U8, name="w1_s", align_bytes=64, offset=8192 + 1024)
-        w2_s = reuse.tile([P, HIDDEN], U8, name="w2_s", align_bytes=64, offset=16384)
+        w1_w = reuse.tile([P, 2 * HIDDEN], U8, name="w1_w", align_bytes=64, offset=8192 + 4096)
+        w2_w = reuse.tile([P, 2 * HIDDEN], U8, name="w2_w", align_bytes=64, offset=16384)
+        w1_s = reuse.tile([P, HIDDEN], U8, name="w1_s", align_bytes=64, offset=8192 + 5120)
+        w2_s = keep.tile([P, HIDDEN], U8, name="w2_s", align_bytes=64)
         e_w = keep.tile([P, PICKED], I32, name="e_w", align_bytes=64)
-        x_w = keep.tile([P, PICKED], I32, name="x_w", align_bytes=64)
+        x_w = reuse.tile([P, PICKED], I32, name="x_w", align_bytes=64, offset=16384)
         e_s = keep.tile([P, PICKED], U8, name="e_s", align_bytes=64)
-        x_s = reuse.tile([P, PICKED], U8, name="x_s", align_bytes=64, offset=16384)
+        x_s = reuse.tile([P, PICKED], U8, name="x_s", align_bytes=64, offset=4096)
 
-        make_identity(nc, identity[:])
-        nc.vector.tensor_reduce(lane[:], identity[:].rearrange("p (g j) -> p j g", j=8), mybir.AxisListType.X, ALU.add)
         deal(nc, w2_w, w2_raw)
         nc.vector.tensor_copy(e_s[:], e_tab_sc[:].indirect(tpl_sb[:]))
         deal(nc, w2_s, w2_raw_sc)
@@ -127,60 +129,85 @@ def tile_picked_yproloc_opn_p_kernel(
 
         ye_ps = first_product("ye_ps", w2_w, w2_s, e_w, e_s)
 
-        picked_units = reuse.tile([P, 2 * PACK, 8], F32, name="picked_units", offset=128)
-        units = keep.tile([P, 2 * PACK], F32, name="units")
+        nc.vector.tensor_copy(x_s[:], x_tab_sc[:].indirect(offs_sb[:]))
+        ye = []
+        gat = [keep.tile([P, PACK, HALF], F32, name="gat%d" % h) for h in range(2)]
+        hid2_rows = [
+            reuse.tile([P, PACK, HALF], BF16, name="hid2_rows0", offset=24576),
+            reuse.tile([P, PACK, HALF], BF16, name="hid2_rows1", offset=8192 + 2048),
+        ]
+
+        def gate(t, h):
+            nc.scalar.activation(gat[h][:, t, :], ye[t][:].indirect(nx_sb[:, 16 * h : 16 * (h + 1)]), ACT.Sigmoid)
+
+        for t in range(PACK):
+            ye.append(keep.tile([P, PICKED], F32, name="ye%d" % (t % 3)))
+            if t < 3:
+                nc.vector.tensor_copy(ye[t][:], ye_ps[t][:])
+            else:
+                nc.scalar.copy(ye[t][:], ye_ps[t][:])
+            gate(t, 0)
+            if t < 2:
+                gate(t, 1)
+        for t in range(2, PACK):
+            gate(t, 1)
+        nc.vector.tensor_copy(x_w[:].bitcast(U32), x_tab[:].bitcast(U32).indirect(offs_sb[:]))
+        deal(nc, w1_w, w1_raw)
+        deal(nc, w1_s, w1_raw_sc)
+        y_ps = first_product("y_ps", w1_w, w1_s, x_w, x_s)
+        picked_units = reuse.tile([P, 2 * PACK, 8], F32, name="picked_units", offset=8192 + 6144)
+        units = keep.tile([P, 2, PACK], F32, name="units")
+        negative = keep.tile([P, PACK], F32, name="negative")
+        signed_units = keep.tile([P, 2, PACK], F32, name="signed_units")
         nc.vector.tensor_tensor(
             picked_units[:],
             unit_blocks[:].rearrange("p w (t j) -> p (w t) j", j=8),
             lane[:].unsqueeze(1).broadcast_to([P, 2 * PACK, 8]),
             ALU.mult,
         )
-        nc.vector.tensor_reduce(units[:], picked_units[:], mybir.AxisListType.X, ALU.add)
-        unit_sb = units[:, :PACK]
-        unit2_sb = units[:, PACK:]
-        unit_abs = reuse.tile([P, PACK], F32, name="unit_abs", offset=0)
-        unit_neg = reuse.tile([P, PACK], F32, name="unit_neg", offset=64)
-        unit2_signed = keep.tile([P, PACK], F32, name="unit2_signed")
-        nc.vector.scalar_tensor_tensor(unit_abs[:], unit_sb, -1.0, unit_sb, ALU.mult, ALU.max)
-        nc.vector.tensor_scalar(unit_neg[:], unit_sb, 0.0, -2.0, ALU.is_lt, ALU.mult)
-        nc.vector.scalar_tensor_tensor(unit2_signed[:], unit_neg[:], 1.0, unit2_sb, ALU.add, ALU.mult)
+        nc.vector.tensor_reduce(units[:].rearrange("p w t -> p (w t)"), picked_units[:], mybir.AxisListType.X, ALU.add)
+        nc.vector.tensor_scalar(negative[:], units[:, 0, :], 0.0, -2.0, ALU.is_lt, ALU.mult)
+        nc.vector.scalar_tensor_tensor(
+            signed_units[:], negative[:].unsqueeze(1).broadcast_to([P, 2, PACK]), 1.0, units[:], ALU.add, ALU.mult
+        )
+        unit_abs = signed_units[:, 0, :]
+        unit2_signed = signed_units[:, 1, :]
 
-
-        ye = [keep.tile([P, PICKED], F32, name="ye%d" % t) for t in range(PACK)]
-        gat = keep.tile([P, PACK, PICKED], F32, name="gat")
-        hid2_rows = reuse.tile([P, PACK, PICKED], BF16, name="hid2_rows", offset=16384 + 512)
-
-        def gate(t):
-            for h in range(2):
-                nc.scalar.activation(
-                    gat[:, t, HALF * h : HALF * (h + 1)],
-                    ye[t][:].indirect(nx_sb[:, 16 * h : 16 * (h + 1)]),
-                    ACT.Sigmoid,
-                )
-
-        nc.vector.tensor_copy(ye[0][:], ye_ps[0][:])
-        gate(0)
-        nc.vector.tensor_copy(ye[1][:], ye_ps[1][:])
-        gate(1)
-        nc.vector.tensor_copy(ye[2][:], ye_ps[2][:])
-        nc.scalar.copy(ye[3][:], ye_ps[3][:])
-        gate(2)
-        gate(3)
-        nc.vector.tensor_copy(x_s[:], x_tab_sc[:].indirect(offs_sb[:]))
-        nc.vector.tensor_copy(x_w[:].bitcast(U32), x_tab[:].bitcast(U32).indirect(offs_sb[:]))
-        deal(nc, w1_w, w1_raw)
-        deal(nc, w1_s, w1_raw_sc)
-        y_ps = first_product("y_ps", w1_w, w1_s, x_w, x_s)
-        for t in range(PACK):
-            nc.vector.scalar_tensor_tensor(
-                hid2_rows[:, t, :], ye_ps[t][:], unit2_signed[:, t : t + 1], gat[:, t, :], ALU.mult, ALU.mult
-            )
-        hid2_bf = keep.tile([P, PICKED, PACK], BF16, name="hid2_bf", align_bytes=64)
-        nc.vector.tensor_copy(hid2_bf[:], hid2_rows[:].rearrange("p t e -> p e t"))
 
         hid2_w = keep.tile([P, PICKED], U32, name="hid2_w", align_bytes=64)
         hid2_s = keep.tile([P, PICKED], U8, name="hid2_s", align_bytes=64)
-        nc.vector.quantize_mx(out=hid2_w[:].bitcast(FP8X4), scales=hid2_s[:], in_=hid2_bf[:].rearrange("p e t -> p (e t)"))
+        hid2_bf = [keep.tile([P, HALF, PACK], BF16, name="hid2_bf%d" % h, align_bytes=64) for h in range(2)]
+
+        def gated(t, h):
+            nc.vector.scalar_tensor_tensor(
+                hid2_rows[h][:, t, :],
+                ye_ps[t][:, HALF * h : HALF * (h + 1)],
+                unit2_signed[:, t : t + 1],
+                gat[h][:, t, :],
+                ALU.mult,
+                ALU.mult,
+            )
+
+        def weave(h):
+            nc.vector.tensor_copy(hid2_bf[h][:], hid2_rows[h][:].rearrange("p t e -> p e t"))
+
+        def quantise(h):
+            cols = slice(HALF * h, HALF * (h + 1))
+            nc.vector.quantize_mx(
+                out=hid2_w[:, cols].bitcast(FP8X4), scales=hid2_s[:, cols], in_=hid2_bf[h][:].rearrange("p e t -> p (e t)")
+            )
+
+        for t in range(2):
+            gated(t, 0)
+            gated(t, 1)
+        gated(2, 0)
+        gated(3, 0)
+        weave(0)
+        gated(2, 1)
+        quantise(0)
+        gated(3, 1)
+        weave(1)
+        quantise(1)
 
         y_bf = [keep.tile([P, 2, PACK, P], BF16, name="y_bf%d" % h) for h in range(2)]
         for h in range(2):
@@ -191,12 +218,12 @@ def tile_picked_yproloc_opn_p_kernel(
                     ACT.Copy,
                     scale=unit_abs[:, t : t + 1],
                 )
-        gap2 = reuse.tile([P, PICKED], F32, name="gap2", offset=0)
+        gap2 = keep.tile([P, PICKED], F32, name="ye0")
         nc.scalar.activation(gap2[:], gap_tab[:].indirect(tpl_sb[:]), ACT.Copy, scale=-2.0)
 
         sc_ps = []
         for h in range(2):
-            hid_rows = keep.tile([P, PACK, P], BF16, name="hid_rows%d" % h)
+            hid_rows = reuse.tile([P, PACK, P], BF16, name="hid_rows%d" % h, offset=8192 + 2048 + 1024 * h)
             hid_bf = keep.tile([P, P, PACK], BF16, name="hid_bf%d" % h, align_bytes=64)
             hid_w = keep.tile([P, P], U32, name="hid_w%d" % h, align_bytes=64)
             hid_s = keep.tile([P, P], U8, name="hid_s%d" % h, align_bytes=64)
@@ -217,13 +244,18 @@ def tile_picked_yproloc_opn_p_kernel(
         floor = [keep.tile([P, PICKED], F32, name="floor%d" % h) for h in range(2)]
         opened = [keep.tile([P, PICKED], F32, name="opened%d" % h) for h in range(2)]
         result = [keep.tile([P, PICKED], F32, name="result%d" % h) for h in range(2)]
-        nc.scalar.copy(sc_sb[0][:, :PICKED], sc_ps[0][:])
-        nc.vector.scalar_tensor_tensor(floor[1][:], gap2[:], 0.5, sc_ps[1][:], ALU.mult, ALU.max)
-        nc.scalar.copy(sc_sb[1][:, :PICKED], sc_ps[1][:])
-        nc.vector.tensor_tensor(opened[0][:], sc_sb[0][:].indirect(dg_sb[:]), gap2[:], ALU.add)
-        nc.vector.scalar_tensor_tensor(floor[0][:], gap2[:], 0.5, sc_ps[0][:], ALU.mult, ALU.max)
-        nc.vector.tensor_tensor(result[0][:], opened[0][:], floor[0][:], ALU.max)
-        nc.sync.dma_start(out=out[0:P, :], in_=result[0][:])
-        nc.vector.tensor_tensor(opened[1][:], sc_sb[1][:].indirect(dg_sb[:]), gap2[:], ALU.add)
-        nc.vector.tensor_tensor(result[1][:], opened[1][:], floor[1][:], ALU.max)
-        nc.sync.dma_start(out=out[P : 2 * P, :], in_=result[1][:])
+        looked = [keep.tile([P, PICKED], F32, name="looked%d" % h) for h in range(2)]
+        for h in range(2):
+            nc.scalar.copy(sc_sb[h][:], sc_ps[h][:])
+            for c in range(2):
+                nc.scalar.activation(
+                    looked[h][:, HALF * c : HALF * (c + 1)], sc_sb[h][:].indirect(dg_sb[:, 16 * c : 16 * (c + 1)]), ACT.Copy
+                )
+        for h in range(2):
+            nc.vector.scalar_tensor_tensor(floor[h][:], gap2[:], 0.5, sc_ps[h][:], ALU.mult, ALU.max)
+        for h in range(2):
+            for c in range(2):
+                cols = slice(HALF * c, HALF * (c + 1))
+                nc.vector.tensor_tensor(opened[h][:, cols], looked[h][:, cols], gap2[:, cols], ALU.add)
+                nc.vector.tensor_tensor(result[h][:, cols], opened[h][:, cols], floor[h][:, cols], ALU.max)
+                nc.sync.dma_start(out=out[P * h : P * (h + 1), cols], in_=result[h][:, cols])

@@ -39,6 +39,13 @@ def load_scale_rows_wrapped(queue, plane, rows):
     queue.dma_start(out=plane[98:P, :].bitcast(I32), in_=words[14:16, :].unsqueeze(0).broadcast_to([15, 2, width]))
 
 
+def weave_rows(nc, woven, rows):
+    nc.vector.tensor_copy(
+        out=woven[:].rearrange("p (c i) t -> p c t i", i=4),
+        in_=rows[:].rearrange("p t (c i) -> p c t i", i=4),
+    )
+
+
 def deal(nc, dealt, raw):
     nc.vector.tensor_copy(
         out=dealt[:].bitcast(I32).rearrange("p (t g w) -> p t g w", t=PACK, g=16),
@@ -64,7 +71,7 @@ def tile_picked_yproloc_opn_p_kernel(
         e_tab_sc = keep.tile([P, TABLE], U8, name="e_tab_sc")
         x_tab_sc = keep.tile([P, TABLE], U8, name="x_tab_sc")
         gap_tab = keep.tile([P, TABLE], F32, name="gap_tab")
-        w1_raw = keep.tile([P, 2 * HIDDEN], U8, name="w1_raw")
+        w1_raw = reuse.tile([P, 2 * HIDDEN], U8, name="w1_raw", offset=24576 + 512)
         w2_raw = keep.tile([P, 2 * HIDDEN], U8, name="w2_raw")
         w1_raw_sc = reuse.tile([P, HIDDEN], U8, name="w1_raw_sc", offset=24576)
         w2_raw_sc = keep.tile([P, HIDDEN], U8, name="w2_raw_sc")
@@ -85,51 +92,54 @@ def tile_picked_yproloc_opn_p_kernel(
         nc.sync.dma_start(out=w2_raw[:].bitcast(I32), in_=w2_words[0].bitcast(I32))
         nc.sync.dma_start(out=e_tab[:], in_=e_words[0].rearrange("p n t -> p (n t)").bitcast(I32))
         for q in range(4):
-            load_scale_rows(nc.sync, x_tab_sc, x_scales[0], q)
-        nc.sync.dma_start(offs_sb[:], offs)
-        nc.sync.dma_start(out=x_tab[:], in_=x_words[0].rearrange("p n t -> p (n t)").bitcast(I32))
-        nc.sync.dma_start(out=w1_raw[:].bitcast(I32), in_=w1_words[0].bitcast(I32))
+            load_scale_rows(nc.sync, w2_raw_sc, w2_scales[0], q)
         for which, factors in enumerate((unit, unit2)):
             blocks = factors.rearrange("(g i) o -> g (i o)", i=32)
             nc.sync.dma_start(out=unit_blocks[:, which, :], in_=blocks.unsqueeze(1).broadcast_to([16, 8, 32]))
+        nc.sync.dma_start(out=x_tab[:], in_=x_words[0].rearrange("p n t -> p (n t)").bitcast(I32))
+        nc.sync.dma_start(offs_sb[:], offs)
+        for q in range(4):
+            load_scale_rows(nc.sync, x_tab_sc, x_scales[0], q)
+        nc.sync.dma_start(out=w1_raw[:].bitcast(I32), in_=w1_words[0].bitcast(I32))
         nc.sync.dma_start(out=gap_tab[:], in_=gap)
         nc.sync.dma_start(dg_sb[:], dg)
-        load_scale_rows_wrapped(nc.gpsimd, w2_raw_sc, w2_scales[0])
         load_scale_rows_wrapped(nc.gpsimd, w1_raw_sc, w1_scales[0])
 
         w1_w = reuse.tile([P, 2 * HIDDEN], U8, name="w1_w", align_bytes=64, offset=8192 + 4096)
         w2_w = reuse.tile([P, 2 * HIDDEN], U8, name="w2_w", align_bytes=64, offset=16384)
         w1_s = reuse.tile([P, HIDDEN], U8, name="w1_s", align_bytes=64, offset=8192 + 5120)
-        w2_s = keep.tile([P, HIDDEN], U8, name="w2_s", align_bytes=64)
+        w2_s = reuse.tile([P, HIDDEN], U8, name="w2_s", align_bytes=64, offset=20480)
         e_w = keep.tile([P, PICKED], I32, name="e_w", align_bytes=64)
         x_w = reuse.tile([P, PICKED], I32, name="x_w", align_bytes=64, offset=16384)
         e_s = keep.tile([P, PICKED], U8, name="e_s", align_bytes=64)
-        x_s = reuse.tile([P, PICKED], U8, name="x_s", align_bytes=64, offset=4096)
+        x_s = reuse.tile([P, PICKED], U8, name="x_s", align_bytes=64, offset=20480)
 
         deal(nc, w2_w, w2_raw)
         nc.vector.tensor_copy(e_s[:], e_tab_sc[:].indirect(tpl_sb[:]))
         deal(nc, w2_s, w2_raw_sc)
-        nc.vector.tensor_copy(e_w[:].bitcast(U32), e_tab[:].bitcast(U32).indirect(tpl_sb[:]))
+        for h in range(2):
+            nc.vector.tensor_copy(
+                e_w[:, HALF * h : HALF * (h + 1)].bitcast(U32), e_tab[:].bitcast(U32).indirect(tpl_sb[:, 16 * h : 16 * (h + 1)])
+            )
 
-        def first_product(name, w_w, w_s, g_w, g_s):
-            banks = []
-            for t in range(PACK):
-                bank = psum.tile([P, PICKED], F32, name="%s%d" % (name, t))
-                nc.tensor.matmul_mx(
-                    out=bank[:],
-                    lhsT=w_w[:, 2 * P * t : 2 * P * (t + 1)].bitcast(FP4X4),
-                    lhsT_scale=w_s[:, P * t : P * (t + 1)],
-                    rhs=g_w[:].bitcast(FP8X4),
-                    rhs_scale=g_s[:],
-                    start=True,
-                    stop=True,
-                )
-                banks.append(bank)
-            return banks
+        def first_product(bank, t, cols, w_w, w_s, g_w, g_s):
+            nc.tensor.matmul_mx(
+                out=bank[:, cols],
+                lhsT=w_w[:, 2 * P * t : 2 * P * (t + 1)].bitcast(FP4X4),
+                lhsT_scale=w_s[:, P * t : P * (t + 1)],
+                rhs=g_w[:, cols].bitcast(FP8X4),
+                rhs_scale=g_s[:, cols],
+                start=True,
+                stop=True,
+            )
 
-        ye_ps = first_product("ye_ps", w2_w, w2_s, e_w, e_s)
+        ye_ps = [psum.tile([P, PICKED], F32, name="ye_ps%d" % t) for t in range(PACK)]
+        for h in range(2):
+            for t in range(2):
+                first_product(ye_ps[t], t, slice(HALF * h, HALF * (h + 1)), w2_w, w2_s, e_w, e_s)
+        for t in range(2, PACK):
+            first_product(ye_ps[t], t, slice(0, PICKED), w2_w, w2_s, e_w, e_s)
 
-        nc.vector.tensor_copy(x_s[:], x_tab_sc[:].indirect(offs_sb[:]))
         ye = []
         gat = [keep.tile([P, PACK, HALF], F32, name="gat%d" % h) for h in range(2)]
         hid2_rows = [
@@ -151,25 +161,32 @@ def tile_picked_yproloc_opn_p_kernel(
                 gate(t, 1)
         for t in range(2, PACK):
             gate(t, 1)
+        nc.vector.tensor_copy(x_s[:], x_tab_sc[:].indirect(offs_sb[:]))
         nc.vector.tensor_copy(x_w[:].bitcast(U32), x_tab[:].bitcast(U32).indirect(offs_sb[:]))
         deal(nc, w1_w, w1_raw)
         deal(nc, w1_s, w1_raw_sc)
-        y_ps = first_product("y_ps", w1_w, w1_s, x_w, x_s)
-        picked_units = reuse.tile([P, 2 * PACK, 8], F32, name="picked_units", offset=8192 + 6144)
+        y_ps = [psum.tile([P, PICKED], F32, name="y_ps%d" % t) for t in range(PACK)]
+        for t in range(PACK):
+            first_product(y_ps[t], t, slice(0, PICKED), w1_w, w1_s, x_w, x_s)
+        picked_units = keep.tile([P, 2 * PACK, 8], F32, name="picked_units")
+        sum4 = keep.tile([P, 2 * PACK, 4], F32, name="sum4")
+        sum2 = keep.tile([P, 2 * PACK, 2], F32, name="sum2")
         units = keep.tile([P, 2, PACK], F32, name="units")
         negative = keep.tile([P, PACK], F32, name="negative")
+        sign = keep.tile([P, PACK], F32, name="sign")
         signed_units = keep.tile([P, 2, PACK], F32, name="signed_units")
-        nc.vector.tensor_tensor(
+        nc.gpsimd.tensor_tensor(
             picked_units[:],
             unit_blocks[:].rearrange("p w (t j) -> p (w t) j", j=8),
             lane[:].unsqueeze(1).broadcast_to([P, 2 * PACK, 8]),
             ALU.mult,
         )
-        nc.vector.tensor_reduce(units[:].rearrange("p w t -> p (w t)"), picked_units[:], mybir.AxisListType.X, ALU.add)
-        nc.vector.tensor_scalar(negative[:], units[:, 0, :], 0.0, -2.0, ALU.is_lt, ALU.mult)
-        nc.vector.scalar_tensor_tensor(
-            signed_units[:], negative[:].unsqueeze(1).broadcast_to([P, 2, PACK]), 1.0, units[:], ALU.add, ALU.mult
-        )
+        nc.gpsimd.tensor_tensor(sum4[:], picked_units[:, :, 0:4], picked_units[:, :, 4:8], ALU.add)
+        nc.gpsimd.tensor_tensor(sum2[:], sum4[:, :, 0:2], sum4[:, :, 2:4], ALU.add)
+        nc.gpsimd.tensor_tensor(units[:].rearrange("p w t -> p (w t)"), sum2[:, :, 0], sum2[:, :, 1], ALU.add)
+        nc.gpsimd.tensor_scalar(negative[:], units[:, 0, :], 0.0, -2.0, ALU.is_lt, ALU.mult)
+        nc.gpsimd.tensor_scalar(sign[:], negative[:], 1.0, 1.0, ALU.add, ALU.mult)
+        nc.gpsimd.tensor_tensor(signed_units[:], units[:], sign[:].unsqueeze(1).broadcast_to([P, 2, PACK]), ALU.mult)
         unit_abs = signed_units[:, 0, :]
         unit2_signed = signed_units[:, 1, :]
 
@@ -189,7 +206,7 @@ def tile_picked_yproloc_opn_p_kernel(
             )
 
         def weave(h):
-            nc.vector.tensor_copy(hid2_bf[h][:], hid2_rows[h][:].rearrange("p t e -> p e t"))
+            weave_rows(nc, hid2_bf[h], hid2_rows[h])
 
         def quantise(h):
             cols = slice(HALF * h, HALF * (h + 1))
@@ -228,7 +245,7 @@ def tile_picked_yproloc_opn_p_kernel(
             hid_w = keep.tile([P, P], U32, name="hid_w%d" % h, align_bytes=64)
             hid_s = keep.tile([P, P], U8, name="hid_s%d" % h, align_bytes=64)
             nc.vector.tensor_tensor(hid_rows[:], y_bf[h][:, 0], y_bf[h][:, 1], ALU.max)
-            nc.vector.tensor_copy(hid_bf[:], hid_rows[:].rearrange("p t v -> p v t"))
+            weave_rows(nc, hid_bf, hid_rows)
             nc.vector.quantize_mx(out=hid_w[:].bitcast(FP8X4), scales=hid_s[:], in_=hid_bf[:].rearrange("p v t -> p (v t)"))
             bank = psum.tile([P, PICKED], F32, name="ye_ps%d" % h)
             nc.tensor.matmul_mx(
@@ -245,14 +262,20 @@ def tile_picked_yproloc_opn_p_kernel(
         opened = [keep.tile([P, PICKED], F32, name="opened%d" % h) for h in range(2)]
         result = [keep.tile([P, PICKED], F32, name="result%d" % h) for h in range(2)]
         looked = [keep.tile([P, PICKED], F32, name="looked%d" % h) for h in range(2)]
-        for h in range(2):
-            nc.scalar.copy(sc_sb[h][:], sc_ps[h][:])
-            for c in range(2):
-                nc.scalar.activation(
-                    looked[h][:, HALF * c : HALF * (c + 1)], sc_sb[h][:].indirect(dg_sb[:, 16 * c : 16 * (c + 1)]), ACT.Copy
-                )
-        for h in range(2):
-            nc.vector.scalar_tensor_tensor(floor[h][:], gap2[:], 0.5, sc_ps[h][:], ALU.mult, ALU.max)
+
+        def look(h, c):
+            nc.scalar.activation(
+                looked[h][:, HALF * c : HALF * (c + 1)], sc_sb[h][:].indirect(dg_sb[:, 16 * c : 16 * (c + 1)]), ACT.Copy
+            )
+
+        nc.scalar.copy(sc_sb[0][:], sc_ps[0][:])
+        nc.vector.scalar_tensor_tensor(floor[1][:], gap2[:], 0.5, sc_ps[1][:], ALU.mult, ALU.max)
+        look(0, 0)
+        nc.scalar.copy(sc_sb[1][:], sc_ps[1][:])
+        nc.vector.scalar_tensor_tensor(floor[0][:], gap2[:], 0.5, sc_ps[0][:], ALU.mult, ALU.max)
+        look(0, 1)
+        look(1, 0)
+        look(1, 1)
         for h in range(2):
             for c in range(2):
                 cols = slice(HALF * c, HALF * (c + 1))

@@ -32,6 +32,10 @@ def load_scale_rows(queue, plane, rows, q):
     )
 
 
+def load_live_scale_rows(queue, plane, rows, q):
+    queue.dma_start(out=plane[32 * q : 32 * q + 4, :].bitcast(I32), in_=rows[4 * q : 4 * q + 4, :].bitcast(I32))
+
+
 def load_scale_rows_wrapped(queue, plane, rows):
     words = rows.bitcast(I32)
     width = words.shape[1]
@@ -81,6 +85,7 @@ def tile_picked_yproloc_opn_p_kernel(
         lane = keep.tile([P, 8], F32, name="lane")
         sc_sb = [keep.tile([P, PICKED], F32, name="sc_sb%d" % h) for h in range(2)]
 
+        nc.vector.memset(x_tab_sc[:].bitcast(I32), 0)
         nc.gpsimd.iota(distance[:], [[-1, 8]], base=8, channel_multiplier=1)
         nc.vector.tensor_scalar(distance8[:], distance[:], 7, None, ALU.bitwise_and)
         nc.vector.tensor_scalar(lane[:], distance8[:], 0.0, None, ALU.is_equal)
@@ -99,7 +104,7 @@ def tile_picked_yproloc_opn_p_kernel(
         nc.sync.dma_start(out=x_tab[:], in_=x_words[0].rearrange("p n t -> p (n t)").bitcast(I32))
         nc.sync.dma_start(offs_sb[:], offs)
         for q in range(4):
-            load_scale_rows(nc.sync, x_tab_sc, x_scales[0], q)
+            load_live_scale_rows(nc.sync, x_tab_sc, x_scales[0], q)
         nc.sync.dma_start(out=w1_raw[:].bitcast(I32), in_=w1_words[0].bitcast(I32))
         nc.sync.dma_start(out=gap_tab[:], in_=gap)
         nc.sync.dma_start(dg_sb[:], dg)
@@ -262,23 +267,15 @@ def tile_picked_yproloc_opn_p_kernel(
         opened = [keep.tile([P, PICKED], F32, name="opened%d" % h) for h in range(2)]
         result = [keep.tile([P, PICKED], F32, name="result%d" % h) for h in range(2)]
         looked = [keep.tile([P, PICKED], F32, name="looked%d" % h) for h in range(2)]
-
-        def look(h, c):
-            nc.scalar.activation(
-                looked[h][:, HALF * c : HALF * (c + 1)], sc_sb[h][:].indirect(dg_sb[:, 16 * c : 16 * (c + 1)]), ACT.Copy
-            )
-
-        nc.scalar.copy(sc_sb[0][:], sc_ps[0][:])
-        nc.vector.scalar_tensor_tensor(floor[1][:], gap2[:], 0.5, sc_ps[1][:], ALU.mult, ALU.max)
-        look(0, 0)
-        nc.scalar.copy(sc_sb[1][:], sc_ps[1][:])
-        nc.vector.scalar_tensor_tensor(floor[0][:], gap2[:], 0.5, sc_ps[0][:], ALU.mult, ALU.max)
-        look(0, 1)
-        look(1, 0)
-        look(1, 1)
         for h in range(2):
+            nc.scalar.copy(sc_sb[h][:], sc_ps[h][:])
             for c in range(2):
-                cols = slice(HALF * c, HALF * (c + 1))
-                nc.vector.tensor_tensor(opened[h][:, cols], looked[h][:, cols], gap2[:, cols], ALU.add)
-                nc.vector.tensor_tensor(result[h][:, cols], opened[h][:, cols], floor[h][:, cols], ALU.max)
-                nc.sync.dma_start(out=out[P * h : P * (h + 1), cols], in_=result[h][:, cols])
+                nc.scalar.activation(
+                    looked[h][:, HALF * c : HALF * (c + 1)], sc_sb[h][:].indirect(dg_sb[:, 16 * c : 16 * (c + 1)]), ACT.Copy
+                )
+        for h in range(2):
+            nc.vector.scalar_tensor_tensor(floor[h][:], gap2[:], 0.5, sc_ps[h][:], ALU.mult, ALU.max)
+        for h, cols in ((0, slice(0, PICKED)), (1, slice(0, HALF)), (1, slice(HALF, PICKED))):
+            nc.vector.tensor_tensor(opened[h][:, cols], looked[h][:, cols], gap2[:, cols], ALU.add)
+            nc.vector.tensor_tensor(result[h][:, cols], opened[h][:, cols], floor[h][:, cols], ALU.max)
+            nc.sync.dma_start(out=out[P * h : P * (h + 1), cols], in_=result[h][:, cols])

@@ -275,7 +275,8 @@ def tile_picked_yproloc_opn_p_kernel(
                 )
         for h in range(2):
             nc.vector.scalar_tensor_tensor(floor[h][:], gap2[:], 0.5, sc_ps[h][:], ALU.mult, ALU.max)
-        for h, cols in ((0, slice(0, PICKED)), (1, slice(0, HALF)), (1, slice(HALF, PICKED))):
+        for h, c in ((0, 0), (0, 1), (1, 0), (1, 1)):
+            cols = slice(HALF * c, HALF * (c + 1))
             nc.vector.tensor_tensor(opened[h][:, cols], looked[h][:, cols], gap2[:, cols], ALU.add)
             nc.vector.tensor_tensor(result[h][:, cols], opened[h][:, cols], floor[h][:, cols], ALU.max)
             nc.sync.dma_start(out=out[P * h : P * (h + 1), cols], in_=result[h][:, cols])

from contextlib import ExitStack

import concourse.mybir as mybir

F32 = mybir.dt.float32
BF16 = mybir.dt.bfloat16
I32 = mybir.dt.int32
U32 = mybir.dt.uint32
U16 = mybir.dt.uint16
U8 = mybir.dt.uint8
FP8X4 = mybir.dt.float8_e4m3fn_x4
FP4X4 = mybir.dt.float4_e2m1fn_x4
ALU = mybir.AluOpType
ACT = mybir.ActivationFunctionType

P = 128
PACK = 4
TABLE = 2048
PICKED = 512
HIDDEN = 512
SEGMENTS = 256
HALF = 256

FLOPS = 2 * 512 * 512 * 512 * 2 + 2 * 512 * 256 * 512


def load_scale_rows(queue, plane, rows, q):
    four = rows[4 * q : 4 * q + 4, :].bitcast(I32)
    queue.dma_start(
        out=plane[32 * q : 32 * q + 32, :].bitcast(I32),
        in_=four.unsqueeze(0).broadcast_to([8, 4, four.shape[1]]),
    )


def load_live_scale_rows(queue, plane, rows, q):
    queue.dma_start(out=plane[32 * q : 32 * q + 4, :].bitcast(I32), in_=rows[4 * q : 4 * q + 4, :].bitcast(I32))


def load_scale_rows_wrapped(queue, plane, rows):
    words = rows.bitcast(I32)
    width = words.shape[1]
    queue.dma_start(out=plane[0:98, :].bitcast(I32), in_=words[0:14, :].unsqueeze(0).broadcast_to([7, 14, width]))
    queue.dma_start(out=plane[98:P, :].bitcast(I32), in_=words[14:16, :].unsqueeze(0).broadcast_to([15, 2, width]))


def weave_rows(nc, woven, rows):
    nc.vector.tensor_copy(
        out=woven[:].rearrange("p (c i) t -> p c t i", i=4),
        in_=rows[:].rearrange("p t (c i) -> p c t i", i=4),
    )


def deal(nc, dealt, raw):
    nc.vector.tensor_copy(
        out=dealt[:].bitcast(I32).rearrange("p (t g w) -> p t g w", t=PACK, g=16),
        in_=raw[:].bitcast(I32).rearrange("p (g t w) -> p t g w", t=PACK, g=16),
    )


def tile_picked_yproloc_opn_p_kernel(
    tc, x_words, x_scales, w1_words, w1_scales, e_words, e_scales, w2_words, w2_scales, unit, unit2, gap, offs, tpl, nx, dg, out
):
    nc = tc.nc
    with ExitStack() as ctx:
        keep = ctx.enter_context(tc.tile_pool(name="keep", bufs=1))
        reuse = ctx.enter_context(tc.tile_pool(name="reuse", bufs=1))
        psum = ctx.enter_context(tc.psum_pool(name="psum", bufs=1))

        offs_sb = keep.tile([P, PICKED // 16], U16, name="offs_sb")
        tpl_sb = keep.tile([P, PICKED // 16], U16, name="tpl_sb")
        nx_sb = keep.tile([P, PICKED // 16], U16, name="nx_sb")
        dg_sb = keep.tile([P, PICKED // 16], U16, name="dg_sb")
        e_tab = reuse.tile([P, TABLE], I32, name="e_tab", offset=0)
        x_tab = reuse.tile([P, TABLE], I32, name="x_tab", offset=8192)
        e_tab_sc = keep.tile([P, TABLE], U8, name="e_tab_sc")
        x_tab_sc = keep.tile([P, TABLE], U8, name="x_tab_sc")
        gap_tab = keep.tile([P, TABLE], F32, name="gap_tab")
        w1_raw = reuse.tile([P, 2 * HIDDEN], U8, name="w1_raw", offset=24576 + 512)
        w2_raw = keep.tile([P, 2 * HIDDEN], U8, name="w2_raw")
        w1_raw_sc = reuse.tile([P, HIDDEN], U8, name="w1_raw_sc", offset=24576)
        w2_raw_sc = keep.tile([P, HIDDEN], U8, name="w2_raw_sc")
        unit_blocks = keep.tile([P, 2, 32], F32, name="unit_blocks")
        distance = keep.tile([P, 8], I32, name="distance")
        distance8 = keep.tile([P, 8], I32, name="distance8")
        lane = keep.tile([P, 8], F32, name="lane")
        sc_sb = [keep.tile([P, PICKED], F32, name="sc_sb%d" % h) for h in range(2)]

        nc.vector.memset(x_tab_sc[:].bitcast(I32), 0)
        nc.gpsimd.iota(distance[:], [[-1, 8]], base=8, channel_multiplier=1)
        nc.vector.tensor_scalar(distance8[:], distance[:], 7, None, ALU.bitwise_and)
        nc.vector.tensor_scalar(lane[:], distance8[:], 0.0, None, ALU.is_equal)

        nc.sync.dma_start(tpl_sb[:], tpl)
        for q in range(4):
            load_scale_rows(nc.sync, e_tab_sc, e_scales[0], q)
        nc.sync.dma_start(nx_sb[:], nx)
        nc.sync.dma_start(out=w2_raw[:].bitcast(I32), in_=w2_words[0].bitcast(I32))
        nc.sync.dma_start(out=e_tab[:], in_=e_words[0].rearrange("p n t -> p (n t)").bitcast(I32))
        for q in range(4):
            load_scale_rows(nc.sync, w2_raw_sc, w2_scales[0], q)
        for which, factors in enumerate((unit, unit2)):
            blocks = factors.rearrange("(g i) o -> g (i o)", i=32)
            nc.sync.dma_start(out=unit_blocks[:, which, :], in_=blocks.unsqueeze(1).broadcast_to([16, 8, 32]))
        nc.sync.dma_start(out=x_tab[:], in_=x_words[0].rearrange("p n t -> p (n t)").bitcast(I32))
        nc.sync.dma_start(offs_sb[:], offs)
        for q in range(4):
            load_live_scale_rows(nc.sync, x_tab_sc, x_scales[0], q)
        nc.sync.dma_start(out=w1_raw[:].bitcast(I32), in_=w1_words[0].bitcast(I32))
        nc.sync.dma_start(out=gap_tab[:], in_=gap)
        nc.sync.dma_start(dg_sb[:], dg)
        load_scale_rows_wrapped(nc.gpsimd, w1_raw_sc, w1_scales[0])

        w1_w = reuse.tile([P, 2 * HIDDEN], U8, name="w1_w", align_bytes=64, offset=8192 + 4096)
        w2_w = reuse.tile([P, 2 * HIDDEN], U8, name="w2_w", align_bytes=64, offset=16384)
        w1_s = reuse.tile([P, HIDDEN], U8, name="w1_s", align_bytes=64, offset=8192 + 5120)
        w2_s = reuse.tile([P, HIDDEN], U8, name="w2_s", align_bytes=64, offset=20480)
        e_w = keep.tile([P, PICKED], I32, name="e_w", align_bytes=64)
        x_w = reuse.tile([P, PICKED], I32, name="x_w", align_bytes=64, offset=16384)
        e_s = keep.tile([P, PICKED], U8, name="e_s", align_bytes=64)
        x_s = reuse.tile([P, PICKED], U8, name="x_s", align_bytes=64, offset=20480)

        deal(nc, w2_w, w2_raw)
        nc.vector.tensor_copy(e_s[:], e_tab_sc[:].indirect(tpl_sb[:]))
        deal(nc, w2_s, w2_raw_sc)
        for h in range(2):
            nc.vector.tensor_copy(
                e_w[:, HALF * h : HALF * (h + 1)].bitcast(U32), e_tab[:].bitcast(U32).indirect(tpl_sb[:, 16 * h : 16 * (h + 1)])
            )

        def first_product(bank, t, cols, w_w, w_s, g_w, g_s):
            nc.tensor.matmul_mx(
                out=bank[:, cols],
                lhsT=w_w[:, 2 * P * t : 2 * P * (t + 1)].bitcast(FP4X4),
                lhsT_scale=w_s[:, P * t : P * (t + 1)],
                rhs=g_w[:, cols].bitcast(FP8X4),
                rhs_scale=g_s[:, cols],
                start=True,
                stop=True,
            )

        ye_ps = [psum.tile([P, PICKED], F32, name="ye_ps%d" % t) for t in range(PACK)]
        for h in range(2):
            for t in range(2):
                first_product(ye_ps[t], t, slice(HALF * h, HALF * (h + 1)), w2_w, w2_s, e_w, e_s)
        for t in range(2, PACK):
            first_product(ye_ps[t], t, slice(0, PICKED), w2_w, w2_s, e_w, e_s)

        ye = []
        gat = [keep.tile([P, PACK, HALF], F32, name="gat%d" % h) for h in range(2)]
        hid2_rows = [
            reuse.tile([P, PACK, HALF], BF16, name="hid2_rows0", offset=24576),
            reuse.tile([P, PACK, HALF], BF16, name="hid2_rows1", offset=8192 + 2048),
        ]

        def gate(t, h):
            nc.scalar.activation(gat[h][:, t, :], ye[t][:].indirect(nx_sb[:, 16 * h : 16 * (h + 1)]), ACT.Sigmoid)

        for t in range(PACK):
            ye.append(keep.tile([P, PICKED], F32, name="ye%d" % (t % 3)))
            if t < 3:
                nc.vector.tensor_copy(ye[t][:], ye_ps[t][:])
            else:
                nc.scalar.copy(ye[t][:], ye_ps[t][:])
            gate(t, 0)
            if t < 2:
                gate(t, 1)
        for t in range(2, PACK):
            gate(t, 1)
        nc.vector.tensor_copy(x_s[:], x_tab_sc[:].indirect(offs_sb[:]))
        nc.vector.tensor_copy(x_w[:].bitcast(U32), x_tab[:].bitcast(U32).indirect(offs_sb[:]))
        deal(nc, w1_w, w1_raw)
        deal(nc, w1_s, w1_raw_sc)
        y_ps = [psum.tile([P, PICKED], F32, name="y_ps%d" % t) for t in range(PACK)]
        for t in range(PACK):
            first_product(y_ps[t], t, slice(0, PICKED), w1_w, w1_s, x_w, x_s)
        picked_units = keep.tile([P, 2 * PACK, 8], F32, name="picked_units")
        sum4 = keep.tile([P, 2 * PACK, 4], F32, name="sum4")
        sum2 = keep.tile([P, 2 * PACK, 2], F32, name="sum2")
        units = keep.tile([P, 2, PACK], F32, name="units")
        negative = keep.tile([P, PACK], F32, name="negative")
        sign = keep.tile([P, PACK], F32, name="sign")
        signed_units = keep.tile([P, 2, PACK], F32, name="signed_units")
        nc.gpsimd.tensor_tensor(
            picked_units[:],
            unit_blocks[:].rearrange("p w (t j) -> p (w t) j", j=8),
            lane[:].unsqueeze(1).broadcast_to([P, 2 * PACK, 8]),
            ALU.mult,
        )
        nc.gpsimd.tensor_tensor(sum4[:], picked_units[:, :, 0:4], picked_units[:, :, 4:8], ALU.add)
        nc.gpsimd.tensor_tensor(sum2[:], sum4[:, :, 0:2], sum4[:, :, 2:4], ALU.add)
        nc.gpsimd.tensor_tensor(units[:].rearrange("p w t -> p (w t)"), sum2[:, :, 0], sum2[:, :, 1], ALU.add)
        nc.gpsimd.tensor_scalar(negative[:], units[:, 0, :], 0.0, -2.0, ALU.is_lt, ALU.mult)
        nc.gpsimd.tensor_scalar(sign[:], negative[:], 1.0, 1.0, ALU.add, ALU.mult)
        nc.gpsimd.tensor_tensor(signed_units[:], units[:], sign[:].unsqueeze(1).broadcast_to([P, 2, PACK]), ALU.mult)
        unit_abs = signed_units[:, 0, :]
        unit2_signed = signed_units[:, 1, :]


        hid2_w = keep.tile([P, PICKED], U32, name="hid2_w", align_bytes=64)
        hid2_s = keep.tile([P, PICKED], U8, name="hid2_s", align_bytes=64)
        hid2_bf = [keep.tile([P, HALF, PACK], BF16, name="hid2_bf%d" % h, align_bytes=64) for h in range(2)]

        def gated(t, h):
            nc.vector.scalar_tensor_tensor(
                hid2_rows[h][:, t, :],
                ye_ps[t][:, HALF * h : HALF * (h + 1)],
                unit2_signed[:, t : t + 1],
                gat[h][:, t, :],
                ALU.mult,
                ALU.mult,
            )

        def weave(h):
            weave_rows(nc, hid2_bf[h], hid2_rows[h])

        def quantise(h):
            cols = slice(HALF * h, HALF * (h + 1))
            nc.vector.quantize_mx(
                out=hid2_w[:, cols].bitcast(FP8X4), scales=hid2_s[:, cols], in_=hid2_bf[h][:].rearrange("p e t -> p (e t)")
            )

        for t in range(2):
            gated(t, 0)
            gated(t, 1)
        gated(2, 0)
        gated(3, 0)
        weave(0)
        gated(2, 1)
        quantise(0)
        gated(3, 1)
        weave(1)
        quantise(1)

        y_bf = [keep.tile([P, 2, PACK, P], BF16, name="y_bf%d" % h) for h in range(2)]
        for h in range(2):
            for t in range(PACK):
                nc.scalar.activation(
                    y_bf[h][:, :, t, :],
                    y_ps[t][:, HALF * h : HALF * (h + 1)].rearrange("p (v d) -> p d v", d=2),
                    ACT.Copy,
                    scale=unit_abs[:, t : t + 1],
                )
        gap2 = keep.tile([P, PICKED], F32, name="ye0")
        nc.scalar.activation(gap2[:], gap_tab[:].indirect(tpl_sb[:]), ACT.Copy, scale=-2.0)

        sc_ps = []
        for h in range(2):
            hid_rows = reuse.tile([P, PACK, P], BF16, name="hid_rows%d" % h, offset=8192 + 2048 + 1024 * h)
            hid_bf = keep.tile([P, P, PACK], BF16, name="hid_bf%d" % h, align_bytes=64)
            hid_w = keep.tile([P, P], U32, name="hid_w%d" % h, align_bytes=64)
            hid_s = keep.tile([P, P], U8, name="hid_s%d" % h, align_bytes=64)
            nc.vector.tensor_tensor(hid_rows[:], y_bf[h][:, 0], y_bf[h][:, 1], ALU.max)
            weave_rows(nc, hid_bf, hid_rows)
            nc.vector.quantize_mx(out=hid_w[:].bitcast(FP8X4), scales=hid_s[:], in_=hid_bf[:].rearrange("p v t -> p (v t)"))
            bank = psum.tile([P, PICKED], F32, name="ye_ps%d" % h)
            nc.tensor.matmul_mx(
                out=bank[:],
                lhsT=hid_w[:].bitcast(FP8X4),
                lhsT_scale=hid_s[:],
                rhs=hid2_w[:].bitcast(FP8X4),
                rhs_scale=hid2_s[:],
                start=True,
                stop=True,
            )
            sc_ps.append(bank)
        floor = [keep.tile([P, PICKED], F32, name="floor%d" % h) for h in range(2)]
        opened = [keep.tile([P, PICKED], F32, name="opened%d" % h) for h in range(2)]
        result = [keep.tile([P, PICKED], F32, name="result%d" % h) for h in range(2)]
        looked = [keep.tile([P, PICKED], F32, name="looked%d" % h) for h in range(2)]
        for h in range(2):
            nc.scalar.copy(sc_sb[h][:], sc_ps[h][:])
            for c in range(2):
                nc.scalar.activation(
                    looked[h][:, HALF * c : HALF * (c + 1)], sc_sb[h][:].indirect(dg_sb[:, 16 * c : 16 * (c + 1)]), ACT.Copy
                )
        for h in range(2):
            nc.vector.scalar_tensor_tensor(floor[h][:], gap2[:], 0.5, sc_ps[h][:], ALU.mult, ALU.max)
        for h, c in ((0, 0), (0, 1), (1, 0), (1, 1)):
            cols = slice(HALF * c, HALF * (c + 1))
            nc.vector.tensor_tensor(opened[h][:, cols], looked[h][:, cols], gap2[:, cols], ALU.add)
            nc.vector.tensor_tensor(result[h][:, cols], opened[h][:, cols], floor[h][:, cols], ALU.max)
            nc.sync.dma_start(out=out[P * h : P * (h + 1), cols], in_=result[h][:, cols])
